import numpy as np
import ml_dtypes


def mxq(x, axis, fmt="e4m3"):
    dtype, down = {"e4m3": (ml_dtypes.float8_e4m3fn, 7), "e5m2": (ml_dtypes.float8_e5m2, 14)}[fmt]
    v = np.moveaxis(np.asarray(x, np.float32).astype(ml_dtypes.bfloat16).astype(np.float64), axis, -1)
    blocks = v.reshape(v.shape[:-1] + (-1, 32))
    amax = np.abs(blocks).max(-1, keepdims=True)
    byte = np.maximum(np.where(amax > 0, np.frexp(amax)[1] - 1 + 127, 0) - down, 1)
    scale = np.exp2(byte - 127.0)
    codes = (blocks / scale).astype(np.float32).astype(dtype).astype(np.float64)
    return np.moveaxis((codes * scale).reshape(v.shape), -1, axis)


WIDE = False


def mx_kscale(k):
    if not WIDE:
        return np.ones(k)
    levels = np.array([10, -10, 5, -5, 0])
    if k % 512:
        return np.exp2(np.random.permutation(np.resize(levels, k // 32))).repeat(32)
    a = np.empty((k // 512, 16))
    for p in range(k // 512):
        a[p, :8] = np.random.permutation(np.resize(levels, 8))
        for g in range(8):
            far = levels[np.abs(levels - a[p, g]) >= 10]
            a[p, g + 8] = far[np.random.randint(len(far))]
    return np.exp2(a.ravel()).repeat(32)


def f64(x):
    return np.asarray(x).astype(np.float64)


def striped(idx):
    return np.tile(np.asarray(idx).reshape(-1, 16).T, (8, 1)).astype(np.uint16)


def unstriped(offs):
    return offs[:16].T.reshape(-1).astype(np.int64)


E2M1 = np.array([0.0, 0.5, 1.0, 1.5, 2.0, 3.0, 4.0, 6.0, -0.0, -0.5, -1.0, -1.5, -2.0, -3.0, -4.0, -6.0])


def pack_weight(w, fmt):
    k, n = w.shape
    w = f64(np.asarray(w, np.float32).astype(ml_dtypes.bfloat16)).reshape(k // 32, 32, n)
    amax = np.abs(w).max(1)
    if fmt == "e4m3":
        byte = np.frexp(amax)[1] - 1 + 127 - 7
    else:
        mant, ex = np.frexp(amax / 6.0)
        byte = np.where(mant > 0.5, ex, ex - 1) + 127
    byte = np.clip(np.where(amax > 0, byte, 1), 1, 254)
    scaled = (w * np.exp2(127.0 - byte)[:, None, :]).reshape(k, n).astype(np.float32)
    by_word = np.ascontiguousarray(scaled.reshape(k // 512, 128, 4, n).transpose(0, 1, 3, 2))
    if fmt == "e4m3":
        words = by_word.astype(ml_dtypes.float8_e4m3fn).view(np.uint8)
    else:
        c = by_word.astype(ml_dtypes.float4_e2m1fn).view(np.uint8) & 0xF
        words = (c[..., 0::2] | (c[..., 1::2] << 4)).reshape(k // 512, 128, 2 * n)
    return np.ascontiguousarray(words), np.ascontiguousarray(byte.astype(np.uint8).reshape(k // 512, 16, n))


def unpack_weight(words, scales, fmt):
    g, _, n = scales.shape
    words = np.ascontiguousarray(words).reshape(g, 128, n, -1)
    if fmt == "e4m3":
        vals = words.view(ml_dtypes.float8_e4m3fn).astype(np.float64)
    else:
        nib = np.empty((g, 128, n, 4), np.uint8)
        nib[..., 0::2] = words & 0xF
        nib[..., 1::2] = words >> 4
        vals = E2M1[nib]
    vals = vals * np.repeat(np.exp2(scales.astype(np.float64) - 127.0), 8, axis=1)[..., None]
    return vals.transpose(0, 1, 3, 2).reshape(g * 512, n)


def sigmoid(v):
    return 1.0 / (1.0 + np.exp(-v))


D, E, T, I, Q = 512, 512, 2048, 512, 128


def setup_inputs():
    n = np.random.standard_normal
    idx = np.random.permutation(T)[:I]
    fd = mx_kscale(D)
    fe = mx_kscale(E)
    fi = mx_kscale(I)
    ti = np.ones(T)
    ti[idx] = fi
    keysp = pack_weight(n((D, T)) / fd[:, None], "e4m3")
    valsp = pack_weight(n((E, T)) / fe[:, None], "e4m3")
    return {
        "query": (n((D, Q)) * 0.8 / np.sqrt(D) * fd[:, None]).astype(np.float32),
        "query2": (n((D, Q)) * 0.8 / np.sqrt(D) * fd[:, None]).astype(np.float32),
        "keys_words": keysp[0],
        "keys_scales": keysp[1],
        "ba": (np.random.uniform(-1.0, 0.5, (Q, 1))).astype(np.float32),
        "bb": (np.random.uniform(-1.0, 0.5, (Q, 1))).astype(np.float32),
        "gout": (n((E, Q)) * 1 / np.sqrt(E) * fe[:, None]).astype(np.float32),
        "vals_words": valsp[0],
        "vals_scales": valsp[1],
        "fs": (np.random.uniform(128.0, 512.0, (1, I)) * fi).astype(np.float32),
        "keyrows": (n((D, T)) / ti).astype(np.float32),
        "res": (n((Q, D)) * 4.0).astype(np.float32),
        "offs": striped(idx),
    }


def reference(query, query2, keys_words, keys_scales, ba, bb, gout, vals_words, vals_scales, fs, keyrows, res, offs):
    idx = unstriped(offs)
    keysu = unpack_weight(keys_words, keys_scales, "e4m3")
    valsu = unpack_weight(vals_words, vals_scales, "e4m3")
    queryq = mxq(f64(query), 0, "e4m3")
    keysidxg = keysu[:, idx]
    a = queryq.T @ keysidxg
    query2q = mxq(f64(query2), 0, "e4m3")
    b = query2q.T @ keysidxg
    u1 = sigmoid(a + f64(ba))
    p = u1 * sigmoid(b + f64(bb))
    w = p / np.sum(p, axis=1, keepdims=True)
    goutq = mxq(f64(gout), 0, "e4m3")
    valsidxg = valsu[:, idx]
    dp = goutq.T @ valsidxg
    ds = w * (dp - np.sum(w * dp, axis=1, keepdims=True)) * (1.0 - u1) * f64(fs)
    dt = ds.T
    kt = f64(keyrows)[:, idx].T
    dtq = mxq(dt, 0, "e4m3")
    ktq = mxq(kt, 0, "e4m3")
    gq = dtq.T @ ktq
    y = gq + f64(res)
    return y

@@ -1,0 +1,202 @@
+from contextlib import ExitStack
+
+import concourse.mybir as mybir
+from concourse.masks import make_identity
+
+D, E, T, I, Q = 512, 512, 2048, 512, 128
+FLOPS = 2 * Q * I * (2 * D + E + D)
+
+F32 = mybir.dt.float32
+BF16 = mybir.dt.bfloat16
+I32 = mybir.dt.int32
+U32 = mybir.dt.uint32
+U16 = mybir.dt.uint16
+U8 = mybir.dt.uint8
+FP8X4 = mybir.dt.float8_e4m3fn_x4
+ALU = mybir.AluOpType
+ACT = mybir.ActivationFunctionType
+
+P = 128
+PACK = 4
+BLOCKS = D // P
+VALS_PLANE = 4
+VECTOR_SLOTS = 288
+SCALAR_ALONE = 2
+
+
+def tile_attend_gbothquestions_kernel(
+    tc, query, query2, keys_words, keys_scales, ba, bb, gout, vals_words, vals_scales, fs, keyrows, res, offs, out
+):
+    nc = tc.nc
+    with ExitStack() as ctx:
+        sb = ctx.enter_context(tc.tile_pool(name="sb", bufs=1))
+        ps = ctx.enter_context(tc.psum_pool(name="ps", bufs=1))
+        ps_turn = ctx.enter_context(tc.psum_pool(name="ps_turn", bufs=2))
+
+        def tile(name, shape, dtype):
+            return sb.tile(shape, dtype, name=name, align_bytes=64)
+
+        offsets = sb.tile([P, I // 16], U16, name="offsets")
+        key_pool = tile("key_pool", [P, T], I32)
+        val_pool = tile("val_pool", [P, T], I32)
+        key_scale_pool = tile("key_scale_pool", [P, T], U8)
+        val_scale_pool = tile("val_scale_pool", [P, T], U8)
+        q_raw = tile("q_raw", [P, PACK, Q], F32)
+        q2_raw = tile("q2_raw", [P, PACK, Q], F32)
+        g_raw = tile("g_raw", [P, PACK, Q], F32)
+        row_pool = [tile("row_pool%d" % j, [P, T], F32) for j in range(BLOCKS)]
+        res_sb = tile("res_sb", [P, D], F32)
+        ba_sb = tile("ba_sb", [P, 1], F32)
+        bb_sb = tile("bb_sb", [P, 1], F32)
+        fs_sb = tile("fs_sb", [P, PACK], F32)
+        ident = tile("ident", [P, P], F32)
+
+        nc.vector.memset(key_scale_pool[:].bitcast(I32), 0)
+        nc.gpsimd.memset(val_scale_pool[:].bitcast(I32), 0)
+        make_identity(nc, ident[:])
+
+        def load_words(dst, words):
+            nc.sync.dma_start(out=dst[:], in_=words[0].rearrange("p n t -> p (n t)").bitcast(I32))
+
+        def load_scales(queue, dst, scales, first):
+            for quad in range(4):
+                queue.dma_start(
+                    out=dst[32 * quad + first : 32 * quad + first + 4, :].bitcast(I32),
+                    in_=scales[0, 4 * quad : 4 * quad + 4, :].bitcast(I32),
+                )
+
+        def load_columns(dst, src):
+            nc.sync.dma_start(out=dst[:], in_=src.rearrange("(p t) q -> p t q", t=PACK))
+
+        def load_rows(j):
+            nc.sync.dma_start(out=row_pool[j][:], in_=keyrows[P * j : P * (j + 1), :])
+
+        load_columns(q_raw, query)
+        load_columns(q2_raw, query2)
+        nc.sync.dma_start(offsets[:], offs)
+        nc.sync.dma_start(out=ba_sb[:], in_=ba)
+        nc.sync.dma_start(out=bb_sb[:], in_=bb)
+        load_words(key_pool, keys_words)
+        nc.sync.dma_start(out=fs_sb[:], in_=fs.rearrange("o (p t) -> p (o t)", t=PACK))
+        load_scales(nc.sync, key_scale_pool, keys_scales, 0)
+        load_words(val_pool, vals_words)
+        load_columns(g_raw, gout)
+        load_scales(nc.sync, val_scale_pool, vals_scales, VALS_PLANE)
+        for j in range(BLOCKS):
+            load_rows(j)
+        nc.sync.dma_start(out=res_sb[:], in_=res)
+
+        def quantize(name, grouped):
+            words = grouped.shape[1] // PACK
+            codes = tile(name + "_codes", [P, words], U32)
+            scales = tile(name + "_scales", [P, words], U8)
+            nc.vector.quantize_mx(out=codes[:].bitcast(FP8X4), scales=scales[:], in_=grouped)
+            return codes, scales
+
+        def product(dst, lhs_codes, lhs_scales, rhs_codes, rhs_scales):
+            nc.tensor.matmul_mx(
+                out=dst,
+                lhsT=lhs_codes.bitcast(FP8X4),
+                lhsT_scale=lhs_scales,
+                rhs=rhs_codes.bitcast(FP8X4),
+                rhs_scale=rhs_scales,
+                start=True,
+                stop=True,
+            )
+
+        def interleave(dst, raw):
+            nc.scalar.copy(out=dst.rearrange("p (q t) -> p q t", t=PACK), in_=raw[:].rearrange("p t q -> p q t"))
+
+        def turn_pairs(name, rows, bank):
+            words = rows[:].bitcast(F32)
+            for u in range(2):
+                nc.tensor.transpose(bank[:, u, :], words[:, u : I // 2 : 2], ident[:])
+            grouped = tile(name + "_grouped", [P, P * PACK], BF16)
+            nc.scalar.copy(
+                out=grouped[:].bitcast(F32).rearrange("p (c u) -> p c u", u=2),
+                in_=bank[:].rearrange("p u c -> p c u"),
+            )
+            return grouped
+
+        key_codes = tile("key_codes", [P, I], U32)
+        key_scales = tile("key_scales", [P, I], U8)
+        nc.vector.tensor_copy(key_codes[:], key_pool[:].bitcast(U32).indirect(offsets[:]))
+        nc.vector.tensor_copy(key_scales[:], key_scale_pool[:].indirect(offsets[:]))
+        qq_grouped = tile("qq_grouped", [P, 2 * Q * PACK], BF16)
+        interleave(qq_grouped[:, 0 : Q * PACK], q_raw)
+        interleave(qq_grouped[:, Q * PACK : 2 * Q * PACK], q2_raw)
+        qq_codes, qq_scales = quantize("qq", qq_grouped[:])
+        a_ps = ps.tile([P, I], F32, name="a_ps", tag="bank_a")
+        b_ps = ps.tile([P, I], F32, name="b_ps", tag="bank_b")
+        product(a_ps[:], qq_codes[:, 0:Q], qq_scales[:, 0:Q], key_codes[:], key_scales[:])
+        product(b_ps[:], qq_codes[:, Q : 2 * Q], qq_scales[:, Q : 2 * Q], key_codes[:], key_scales[:])
+
+        fs_ps = ps.tile([P, PACK, P], F32, name="fs_ps")
+        for t in range(PACK):
+            nc.tensor.transpose(fs_ps[:, t, :], fs_sb[:, t : t + 1].to_broadcast([P, P]), ident[:])
+
+        neg_ba = tile("neg_ba", [P, 1], F32)
+        nc.vector.tensor_scalar(neg_ba[:], ba_sb[:], -1.0, None, ALU.mult)
+        u1 = tile("u1", [P, I], F32)
+        u2 = tile("u2", [P, I], F32)
+        rest1 = tile("rest1", [P, I], F32)
+        nc.scalar.activation(u1[:], a_ps[:], ACT.Sigmoid, bias=ba_sb[:])
+        nc.scalar.activation(u2[:], b_ps[:], ACT.Sigmoid, bias=bb_sb[:])
+        nc.scalar.activation(rest1[:], a_ps[:], ACT.Sigmoid, bias=neg_ba[:], scale=-1.0)
+
+        val_codes = tile("val_codes", [P, I], U32)
+        val_scales = tile("val_scales", [P, I], U8)
+        nc.vector.tensor_copy(val_codes[:], val_pool[:].bitcast(U32).indirect(offsets[:]))
+        nc.vector.tensor_copy(val_scales[:], val_scale_pool[:].indirect(offsets[:]))
+        g_grouped = tile("g_grouped", [P, Q * PACK], BF16)
+        interleave(g_grouped[:], g_raw)
+        g_codes, g_scales = quantize("g", g_grouped[:])
+        dp_ps = ps.tile([P, I], F32, name="dp_ps")
+        product(dp_ps[:], g_codes[:], g_scales[:], val_codes[:], val_scales[VALS_PLANE:P, :])
+
+        pw = tile("pw", [P, I], F32)
+        p_sum = tile("p_sum", [P, 1], F32)
+        inv_sum = tile("inv_sum", [P, 1], F32)
+        rest_fs = tile("rest_fs", [P, I], F32)
+        factor = tile("factor", [P, I], F32)
+        w_dp = tile("w_dp", [P, I], F32)
+        mean_dp = tile("mean_dp", [P, 1], F32)
+        ds = tile("ds", [P, I], BF16)
+        nc.vector.scalar_tensor_tensor(pw[:], u1[:], 1.0, u2[:], ALU.mult, ALU.mult, accum_out=p_sum[:])
+        nc.vector.tensor_tensor(
+            rest_fs[:].rearrange("p (s t) -> p s t", t=PACK),
+            rest1[:].rearrange("p (s t) -> p s t", t=PACK),
+            fs_ps[:].rearrange("p t s -> p s t"),
+            ALU.mult,
+        )
+        nc.vector.reciprocal(inv_sum[:], p_sum[:])
+        nc.vector.scalar_tensor_tensor(w_dp[:], dp_ps[:], inv_sum[:], pw[:], ALU.mult, ALU.mult, accum_out=mean_dp[:])
+        nc.vector.scalar_tensor_tensor(factor[:], pw[:], inv_sum[:], rest_fs[:], ALU.mult, ALU.mult)
+        nc.vector.scalar_tensor_tensor(ds[:], dp_ps[:], mean_dp[:], factor[:], ALU.subtract, ALU.mult)
+        ds_bank = ps.tile([P, 2, P], F32, name="ds_bank", tag="bank_a")
+        dt_codes, dt_scales = quantize("dt", turn_pairs("dt", ds, ds_bank)[:])
+
+        early = P * (BLOCKS - 1)
+        gq_early = ps.tile([P, early], F32, name="gq_early")
+        gq_last = ps.tile([P, P], F32, name="gq_last", tag="bank_b")
+        for j in range(BLOCKS):
+            picked = tile("picked%d" % j, [P, I], BF16)
+            gq = gq_early[:, P * j : P * (j + 1)] if j < BLOCKS - 1 else gq_last[:]
+            if j < SCALAR_ALONE:
+                nc.scalar.activation(picked[:], row_pool[j][:].indirect(offsets[:]), ACT.Copy)
+            else:
+                cut = VECTOR_SLOTS // 16
+                nc.vector.tensor_copy(picked[:, 0:VECTOR_SLOTS], row_pool[j][:].indirect(offsets[:, 0:cut]))
+                nc.scalar.activation(
+                    picked[:, VECTOR_SLOTS:I], row_pool[j][:].indirect(offsets[:, cut : I // 16]), ACT.Copy
+                )
+            bank = ps_turn.tile([P, 2, P], F32, name="kt_bank")
+            kt_codes, kt_scales = quantize("kt%d" % j, turn_pairs("kt%d" % j, picked, bank)[:])
+            product(gq, dt_codes[:], dt_scales[:], kt_codes[:], kt_scales[:])
+
+        y_early = tile("y_early", [P, early], F32)
+        y_last = tile("y_last", [P, P], F32)
+        nc.vector.tensor_tensor(y_early[:], gq_early[:], res_sb[:, 0:early], ALU.add)
+        nc.sync.dma_start(out=out[:, 0:early], in_=y_early[:])
+        nc.vector.tensor_tensor(y_last[:], gq_last[:], res_sb[:, early:D], ALU.add)
+        nc.sync.dma_start(out=out[:, early:D], in_=y_last[:])

@@ -21,7 +21,6 @@ PACK = 4
 BLOCKS = D // P
 VALS_PLANE = 4
 VECTOR_SLOTS = 288
-SCALAR_ALONE = 2
 
 
 def tile_attend_gbothquestions_kernel(
@@ -33,62 +32,37 @@ def tile_attend_gbothquestions_kernel(
         ps = ctx.enter_context(tc.psum_pool(name="ps", bufs=1))
         ps_turn = ctx.enter_context(tc.psum_pool(name="ps_turn", bufs=2))
 
-        def tile(name, shape, dtype):
-            return sb.tile(shape, dtype, name=name, align_bytes=64)
+        def tile(name, shape, dtype, slot=None):
+            return sb.tile(shape, dtype, name=name, tag=slot or name, align_bytes=64)
 
-        offsets = sb.tile([P, I // 16], U16, name="offsets")
-        key_pool = tile("key_pool", [P, T], I32)
-        val_pool = tile("val_pool", [P, T], I32)
-        key_scale_pool = tile("key_scale_pool", [P, T], U8)
-        val_scale_pool = tile("val_scale_pool", [P, T], U8)
-        q_raw = tile("q_raw", [P, PACK, Q], F32)
-        q2_raw = tile("q2_raw", [P, PACK, Q], F32)
-        g_raw = tile("g_raw", [P, PACK, Q], F32)
-        row_pool = [tile("row_pool%d" % j, [P, T], F32) for j in range(BLOCKS)]
-        res_sb = tile("res_sb", [P, D], F32)
-        ba_sb = tile("ba_sb", [P, 1], F32)
-        bb_sb = tile("bb_sb", [P, 1], F32)
-        fs_sb = tile("fs_sb", [P, PACK], F32)
-        ident = tile("ident", [P, P], F32)
+        def load_words(name, words, slot):
+            pool = tile(name, [P, T], I32, slot)
+            nc.sync.dma_start(out=pool[:], in_=words[0].rearrange("p n t -> p (n t)").bitcast(I32))
+            return pool
 
-        nc.vector.memset(key_scale_pool[:].bitcast(I32), 0)
-        nc.gpsimd.memset(val_scale_pool[:].bitcast(I32), 0)
-        make_identity(nc, ident[:])
-
-        def load_words(dst, words):
-            nc.sync.dma_start(out=dst[:], in_=words[0].rearrange("p n t -> p (n t)").bitcast(I32))
-
-        def load_scales(queue, dst, scales, first):
+        def load_scales(name, scales, first, slot, clear):
+            pool = tile(name, [P, T], U8, slot)
+            clear(pool[:].bitcast(I32), 0)
             for quad in range(4):
-                queue.dma_start(
-                    out=dst[32 * quad + first : 32 * quad + first + 4, :].bitcast(I32),
+                nc.sync.dma_start(
+                    out=pool[32 * quad + first : 32 * quad + first + 4, :].bitcast(I32),
                     in_=scales[0, 4 * quad : 4 * quad + 4, :].bitcast(I32),
                 )
+            return pool
 
-        def load_columns(dst, src):
-            nc.sync.dma_start(out=dst[:], in_=src.rearrange("(p t) q -> p t q", t=PACK))
+        def load_columns(name, src, slot):
+            raw = tile(name, [P, PACK, Q], F32, slot)
+            nc.sync.dma_start(out=raw[:], in_=src.rearrange("(p t) q -> p t q", t=PACK))
+            return raw
 
-        def load_rows(j):
-            nc.sync.dma_start(out=row_pool[j][:], in_=keyrows[P * j : P * (j + 1), :])
+        def load_rows(j, slot):
+            rows = tile("row_pool%d" % j, [P, T], F32, slot)
+            nc.sync.dma_start(out=rows[:], in_=keyrows[P * j : P * (j + 1), :])
+            return rows
 
-        load_columns(q_raw, query)
-        load_columns(q2_raw, query2)
-        nc.sync.dma_start(offsets[:], offs)
-        nc.sync.dma_start(out=ba_sb[:], in_=ba)
-        nc.sync.dma_start(out=bb_sb[:], in_=bb)
-        load_words(key_pool, keys_words)
-        nc.sync.dma_start(out=fs_sb[:], in_=fs.rearrange("o (p t) -> p (o t)", t=PACK))
-        load_scales(nc.sync, key_scale_pool, keys_scales, 0)
-        load_words(val_pool, vals_words)
-        load_columns(g_raw, gout)
-        load_scales(nc.sync, val_scale_pool, vals_scales, VALS_PLANE)
-        for j in range(BLOCKS):
-            load_rows(j)
-        nc.sync.dma_start(out=res_sb[:], in_=res)
-
-        def quantize(name, grouped):
+        def quantize(name, grouped, slot=None):
             words = grouped.shape[1] // PACK
-            codes = tile(name + "_codes", [P, words], U32)
+            codes = tile(name + "_codes", [P, words], U32, slot)
             scales = tile(name + "_scales", [P, words], U8)
             nc.vector.quantize_mx(out=codes[:].bitcast(FP8X4), scales=scales[:], in_=grouped)
             return codes, scales
@@ -105,38 +79,64 @@ def tile_attend_gbothquestions_kernel(
             )
 
         def interleave(dst, raw):
-            nc.scalar.copy(out=dst.rearrange("p (q t) -> p q t", t=PACK), in_=raw[:].rearrange("p t q -> p q t"))
+            nc.vector.tensor_copy(out=dst.rearrange("p (q t) -> p q t", t=PACK), in_=raw[:].rearrange("p t q -> p q t"))
 
-        def turn_pairs(name, rows, bank):
+        def turn_pairs(name, rows, copy, slot):
+            bank = ps_turn.tile([P, 2, P], F32, name="turn_bank")
             words = rows[:].bitcast(F32)
             for u in range(2):
                 nc.tensor.transpose(bank[:, u, :], words[:, u : I // 2 : 2], ident[:])
-            grouped = tile(name + "_grouped", [P, P * PACK], BF16)
-            nc.scalar.copy(
+            grouped = tile(name + "_grouped", [P, P * PACK], BF16, slot)
+            copy(
                 out=grouped[:].bitcast(F32).rearrange("p (c u) -> p c u", u=2),
                 in_=bank[:].rearrange("p u c -> p c u"),
             )
             return grouped
 
-        key_codes = tile("key_codes", [P, I], U32)
-        key_scales = tile("key_scales", [P, I], U8)
-        nc.vector.tensor_copy(key_codes[:], key_pool[:].bitcast(U32).indirect(offsets[:]))
-        nc.vector.tensor_copy(key_scales[:], key_scale_pool[:].indirect(offsets[:]))
-        qq_grouped = tile("qq_grouped", [P, 2 * Q * PACK], BF16)
+        q_raw = load_columns("q_raw", query, "slot_a")
+        q2_raw = load_columns("q2_raw", query2, "slot_b")
+        g_raw = load_columns("g_raw", gout, "slot_c")
+        offsets = sb.tile([P, I // 16], U16, name="offsets")
+        nc.sync.dma_start(offsets[:], offs)
+        ba_sb = tile("ba_sb", [P, 1], F32)
+        bb_sb = tile("bb_sb", [P, 1], F32)
+        fs_sb = tile("fs_sb", [P, PACK], F32)
+        nc.sync.dma_start(out=ba_sb[:], in_=ba)
+        nc.sync.dma_start(out=bb_sb[:], in_=bb)
+        key_pool = load_words("key_pool", keys_words, "slot_d")
+        nc.sync.dma_start(out=fs_sb[:], in_=fs.rearrange("o (p t) -> p (o t)", t=PACK))
+        key_scale_pool = load_scales("key_scale_pool", keys_scales, 0, "slot_e", nc.gpsimd.memset)
+        ident = tile("ident", [P, P], F32)
+        make_identity(nc, ident[:])
+
+        qq_grouped = tile("qq_grouped", [P, 2 * Q * PACK], BF16, "slot_f")
+        g_grouped = tile("g_grouped", [P, Q * PACK], BF16, "slot_g")
         interleave(qq_grouped[:, 0 : Q * PACK], q_raw)
+        val_pool = load_words("val_pool", vals_words, "slot_a")
         interleave(qq_grouped[:, Q * PACK : 2 * Q * PACK], q2_raw)
-        qq_codes, qq_scales = quantize("qq", qq_grouped[:])
-        a_ps = ps.tile([P, I], F32, name="a_ps", tag="bank_a")
-        b_ps = ps.tile([P, I], F32, name="b_ps", tag="bank_b")
+        val_scale_pool = load_scales("val_scale_pool", vals_scales, VALS_PLANE, "slot_b", nc.vector.memset)
+        interleave(g_grouped[:], g_raw)
+        qq_codes, qq_scales = quantize("qq", qq_grouped[:], "slot_h")
+        row_pool = [load_rows(0, "slot_f")]
+        g_codes, g_scales = quantize("g", g_grouped[:], "slot_i")
+        neg_ba = tile("neg_ba", [P, 1], F32, "slot_j")
+        nc.vector.tensor_scalar(neg_ba[:], ba_sb[:], -1.0, None, ALU.mult)
+
+        key_codes = tile("key_codes", [P, I], U32, "slot_c")
+        key_scales = tile("key_scales", [P, I], U8, "slot_g")
+        nc.vector.tensor_copy(key_codes[:], key_pool[:].bitcast(U32).indirect(offsets[:]))
+        row_pool.append(load_rows(1, "slot_d"))
+        nc.vector.tensor_copy(key_scales[:], key_scale_pool[:].indirect(offsets[:]))
+        a_ps = ps.tile([P, I], F32, name="a_ps")
+        b_ps = ps.tile([P, I], F32, name="b_ps")
         product(a_ps[:], qq_codes[:, 0:Q], qq_scales[:, 0:Q], key_codes[:], key_scales[:])
         product(b_ps[:], qq_codes[:, Q : 2 * Q], qq_scales[:, Q : 2 * Q], key_codes[:], key_scales[:])
+        row_pool.append(load_rows(2, "slot_h"))
 
         fs_ps = ps.tile([P, PACK, P], F32, name="fs_ps")
         for t in range(PACK):
             nc.tensor.transpose(fs_ps[:, t, :], fs_sb[:, t : t + 1].to_broadcast([P, P]), ident[:])
 
-        neg_ba = tile("neg_ba", [P, 1], F32)
-        nc.vector.tensor_scalar(neg_ba[:], ba_sb[:], -1.0, None, ALU.mult)
         u1 = tile("u1", [P, I], F32)
         u2 = tile("u2", [P, I], F32)
         rest1 = tile("rest1", [P, I], F32)
@@ -145,44 +145,40 @@ def tile_attend_gbothquestions_kernel(
         nc.scalar.activation(rest1[:], a_ps[:], ACT.Sigmoid, bias=neg_ba[:], scale=-1.0)
 
         val_codes = tile("val_codes", [P, I], U32)
-        val_scales = tile("val_scales", [P, I], U8)
+        val_scales = tile("val_scales", [P, I], U8, "slot_e")
         nc.vector.tensor_copy(val_codes[:], val_pool[:].bitcast(U32).indirect(offsets[:]))
+        row_pool.append(load_rows(3, "slot_a"))
         nc.vector.tensor_copy(val_scales[:], val_scale_pool[:].indirect(offsets[:]))
-        g_grouped = tile("g_grouped", [P, Q * PACK], BF16)
-        interleave(g_grouped[:], g_raw)
-        g_codes, g_scales = quantize("g", g_grouped[:])
         dp_ps = ps.tile([P, I], F32, name="dp_ps")
         product(dp_ps[:], g_codes[:], g_scales[:], val_codes[:], val_scales[VALS_PLANE:P, :])
+        res_sb = tile("res_sb", [P, D], F32, "slot_i")
+        nc.sync.dma_start(out=res_sb[:], in_=res)
 
-        pw = tile("pw", [P, I], F32)
+        pw = tile("pw", [P, I], F32, "slot_b")
         p_sum = tile("p_sum", [P, 1], F32)
         inv_sum = tile("inv_sum", [P, 1], F32)
-        rest_fs = tile("rest_fs", [P, I], F32)
-        factor = tile("factor", [P, I], F32)
+        p_rest = tile("p_rest", [P, I], F32)
+        factor = tile("factor", [P, I], F32, "slot_k")
         w_dp = tile("w_dp", [P, I], F32)
         mean_dp = tile("mean_dp", [P, 1], F32)
-        ds = tile("ds", [P, I], BF16)
+        ds = tile("ds", [P, I], BF16, "slot_l")
         nc.vector.scalar_tensor_tensor(pw[:], u1[:], 1.0, u2[:], ALU.mult, ALU.mult, accum_out=p_sum[:])
-        nc.vector.tensor_tensor(
-            rest_fs[:].rearrange("p (s t) -> p s t", t=PACK),
-            rest1[:].rearrange("p (s t) -> p s t", t=PACK),
-            fs_ps[:].rearrange("p t s -> p s t"),
-            ALU.mult,
-        )
+        nc.vector.tensor_tensor(p_rest[:], pw[:], rest1[:], ALU.mult)
         nc.vector.reciprocal(inv_sum[:], p_sum[:])
         nc.vector.scalar_tensor_tensor(w_dp[:], dp_ps[:], inv_sum[:], pw[:], ALU.mult, ALU.mult, accum_out=mean_dp[:])
-        nc.vector.scalar_tensor_tensor(factor[:], pw[:], inv_sum[:], rest_fs[:], ALU.mult, ALU.mult)
+        nc.vector.scalar_tensor_tensor(
+            factor[:].rearrange("p (s t) -> p s t", t=PACK),
+            p_rest[:].rearrange("p (s t) -> p s t", t=PACK),
+            inv_sum[:],
+            fs_ps[:].rearrange("p t s -> p s t"),
+            ALU.mult,
+            ALU.mult,
+        )
         nc.vector.scalar_tensor_tensor(ds[:], dp_ps[:], mean_dp[:], factor[:], ALU.subtract, ALU.mult)
-        ds_bank = ps.tile([P, 2, P], F32, name="ds_bank", tag="bank_a")
-        dt_codes, dt_scales = quantize("dt", turn_pairs("dt", ds, ds_bank)[:])
 
-        early = P * (BLOCKS - 1)
-        gq_early = ps.tile([P, early], F32, name="gq_early")
-        gq_last = ps.tile([P, P], F32, name="gq_last", tag="bank_b")
-        for j in range(BLOCKS):
-            picked = tile("picked%d" % j, [P, I], BF16)
-            gq = gq_early[:, P * j : P * (j + 1)] if j < BLOCKS - 1 else gq_last[:]
-            if j < SCALAR_ALONE:
+        def pick_rows(j, slot):
+            picked = tile("picked%d" % j, [P, I], BF16, slot)
+            if j < BLOCKS - 1:
                 nc.scalar.activation(picked[:], row_pool[j][:].indirect(offsets[:]), ACT.Copy)
             else:
                 cut = VECTOR_SLOTS // 16
@@ -190,9 +186,23 @@ def tile_attend_gbothquestions_kernel(
                 nc.scalar.activation(
                     picked[:, VECTOR_SLOTS:I], row_pool[j][:].indirect(offsets[:, cut : I // 16]), ACT.Copy
                 )
-            bank = ps_turn.tile([P, 2, P], F32, name="kt_bank")
-            kt_codes, kt_scales = quantize("kt%d" % j, turn_pairs("kt%d" % j, picked, bank)[:])
-            product(gq, dt_codes[:], dt_scales[:], kt_codes[:], kt_scales[:])
+            return picked
+
+        picked0 = pick_rows(0, "slot_j")
+        picked1 = pick_rows(1, None)
+        kt = [quantize("kt0", turn_pairs("kt0", picked0, nc.scalar.copy, "slot_d")[:], "slot_k")]
+        dt_codes, dt_scales = quantize("dt", turn_pairs("dt", ds, nc.vector.tensor_copy, "slot_l")[:])
+        picked2 = pick_rows(2, "slot_j")
+        kt.append(quantize("kt1", turn_pairs("kt1", picked1, nc.scalar.copy, "slot_h")[:], "slot_l"))
+        picked3 = pick_rows(3, "slot_h")
+        kt.append(quantize("kt2", turn_pairs("kt2", picked2, nc.scalar.copy, "slot_a")[:]))
+        kt.append(quantize("kt3", turn_pairs("kt3", picked3, nc.scalar.copy, None)[:]))
+        early = P * (BLOCKS - 1)
+        gq_early = ps.tile([P, early], F32, name="gq_early")
+        gq_last = ps.tile([P, P], F32, name="gq_last")
+        for j in range(BLOCKS):
+            gq = gq_early[:, P * j : P * (j + 1)] if j < BLOCKS - 1 else gq_last[:]
+            product(gq, dt_codes[:], dt_scales[:], kt[j][0][:], kt[j][1][:])
 
         y_early = tile("y_early", [P, early], F32)
         y_last = tile("y_last", [P, P], F32)

@@ -30,7 +30,6 @@ def tile_attend_gbothquestions_kernel(
     with ExitStack() as ctx:
         sb = ctx.enter_context(tc.tile_pool(name="sb", bufs=1))
         ps = ctx.enter_context(tc.psum_pool(name="ps", bufs=1))
-        ps_turn = ctx.enter_context(tc.psum_pool(name="ps_turn", bufs=2))
 
         def tile(name, shape, dtype, slot=None):
             return sb.tile(shape, dtype, name=name, tag=slot or name, align_bytes=64)
@@ -43,10 +42,10 @@ def tile_attend_gbothquestions_kernel(
         def load_scales(name, scales, first, slot, clear):
             pool = tile(name, [P, T], U8, slot)
             clear(pool[:].bitcast(I32), 0)
-            for quad in range(4):
+            for r in range(4):
                 nc.sync.dma_start(
-                    out=pool[32 * quad + first : 32 * quad + first + 4, :].bitcast(I32),
-                    in_=scales[0, 4 * quad : 4 * quad + 4, :].bitcast(I32),
+                    out=pool[first + r : P : 32, :].bitcast(I32),
+                    in_=scales[0, r:16:4, :].bitcast(I32),
                 )
             return pool
 
@@ -79,10 +78,13 @@ def tile_attend_gbothquestions_kernel(
             )
 
         def interleave(dst, raw):
-            nc.vector.tensor_copy(out=dst.rearrange("p (q t) -> p q t", t=PACK), in_=raw[:].rearrange("p t q -> p q t"))
+            nc.vector.tensor_copy(
+                out=dst.rearrange("p (c i t) -> p c t i", i=4, t=PACK),
+                in_=raw[:].rearrange("p t (c i) -> p c t i", i=4),
+            )
 
-        def turn_pairs(name, rows, copy, slot):
-            bank = ps_turn.tile([P, 2, P], F32, name="turn_bank")
+        def turn_pairs(name, rows, bank_tag, copy, slot):
+            bank = ps.tile([P, 2, P], F32, name=name + "_bank", tag=bank_tag)
             words = rows[:].bitcast(F32)
             for u in range(2):
                 nc.tensor.transpose(bank[:, u, :], words[:, u : I // 2 : 2], ident[:])
@@ -127,8 +129,8 @@ def tile_attend_gbothquestions_kernel(
         nc.vector.tensor_copy(key_codes[:], key_pool[:].bitcast(U32).indirect(offsets[:]))
         row_pool.append(load_rows(1, "slot_d"))
         nc.vector.tensor_copy(key_scales[:], key_scale_pool[:].indirect(offsets[:]))
-        a_ps = ps.tile([P, I], F32, name="a_ps")
-        b_ps = ps.tile([P, I], F32, name="b_ps")
+        a_ps = ps.tile([P, I], F32, name="a_ps", tag="bank_a")
+        b_ps = ps.tile([P, I], F32, name="b_ps", tag="bank_b")
         product(a_ps[:], qq_codes[:, 0:Q], qq_scales[:, 0:Q], key_codes[:], key_scales[:])
         product(b_ps[:], qq_codes[:, Q : 2 * Q], qq_scales[:, Q : 2 * Q], key_codes[:], key_scales[:])
         row_pool.append(load_rows(2, "slot_h"))
@@ -189,24 +191,27 @@ def tile_attend_gbothquestions_kernel(
             return picked
 
         picked0 = pick_rows(0, "slot_j")
-        picked1 = pick_rows(1, None)
-        kt = [quantize("kt0", turn_pairs("kt0", picked0, nc.scalar.copy, "slot_d")[:], "slot_k")]
-        dt_codes, dt_scales = quantize("dt", turn_pairs("dt", ds, nc.vector.tensor_copy, "slot_l")[:])
-        picked2 = pick_rows(2, "slot_j")
-        kt.append(quantize("kt1", turn_pairs("kt1", picked1, nc.scalar.copy, "slot_h")[:], "slot_l"))
-        picked3 = pick_rows(3, "slot_h")
-        kt.append(quantize("kt2", turn_pairs("kt2", picked2, nc.scalar.copy, "slot_a")[:]))
-        kt.append(quantize("kt3", turn_pairs("kt3", picked3, nc.scalar.copy, None)[:]))
-        early = P * (BLOCKS - 1)
-        gq_early = ps.tile([P, early], F32, name="gq_early")
-        gq_last = ps.tile([P, P], F32, name="gq_last")
-        for j in range(BLOCKS):
-            gq = gq_early[:, P * j : P * (j + 1)] if j < BLOCKS - 1 else gq_last[:]
-            product(gq, dt_codes[:], dt_scales[:], kt[j][0][:], kt[j][1][:])
-
-        y_early = tile("y_early", [P, early], F32)
+        picked1 = pick_rows(1, "slot_m")
+        kt = [quantize("kt0", turn_pairs("kt0", picked0, "bank_x", nc.scalar.copy, "slot_d")[:], "slot_k")]
+        kt1_grouped = turn_pairs("kt1", picked1, "bank_y", nc.scalar.copy, "slot_n")
+        picked2 = pick_rows(2, "slot_m")
+        dt_codes, dt_scales = quantize("dt", turn_pairs("dt", ds, "bank_z", nc.vector.tensor_copy, "slot_l")[:])
+        kt.append(quantize("kt1", kt1_grouped[:], "slot_l"))
+        picked3 = pick_rows(3, "slot_n")
+        kt.append(quantize("kt2", turn_pairs("kt2", picked2, "bank_z", nc.scalar.copy, "slot_a")[:]))
+        kt.append(quantize("kt3", turn_pairs("kt3", picked3, "bank_x", nc.scalar.copy, None)[:]))
+        y_early = tile("y_early", [P, (BLOCKS - 1) * P], F32)
         y_last = tile("y_last", [P, P], F32)
-        nc.vector.tensor_tensor(y_early[:], gq_early[:], res_sb[:, 0:early], ALU.add)
-        nc.sync.dma_start(out=out[:, 0:early], in_=y_early[:])
-        nc.vector.tensor_tensor(y_last[:], gq_last[:], res_sb[:, early:D], ALU.add)
-        nc.sync.dma_start(out=out[:, early:D], in_=y_last[:])
+        groups = [
+            (0, 2, "bank_c", y_early[:, 0 : 2 * P]),
+            (2, 3, "bank_b", y_early[:, 2 * P : 3 * P]),
+            (3, 4, "bank_a", y_last[:]),
+        ]
+        for first, end, bank_tag, y in groups:
+            gq = ps.tile([P, (end - first) * P], F32, name="gq%d" % first, tag=bank_tag)
+            for j in range(first, end):
+                cols = slice((j - first) * P, (j - first + 1) * P)
+                product(gq[:, cols], dt_codes[:], dt_scales[:], kt[j][0][:], kt[j][1][:])
+            nc.vector.tensor_tensor(y, gq[:], res_sb[:, first * P : end * P], ALU.add)
+        nc.sync.dma_start(out=out[:, 0 : (BLOCKS - 1) * P], in_=y_early[:])
+        nc.sync.dma_start(out=out[:, (BLOCKS - 1) * P : D], in_=y_last[:])

from contextlib import ExitStack

import concourse.mybir as mybir
from concourse.masks import make_identity

D, E, T, I, Q = 512, 512, 2048, 512, 128
FLOPS = 2 * Q * I * (2 * D + E + D)

F32 = mybir.dt.float32
BF16 = mybir.dt.bfloat16
I32 = mybir.dt.int32
U32 = mybir.dt.uint32
U16 = mybir.dt.uint16
U8 = mybir.dt.uint8
FP8X4 = mybir.dt.float8_e4m3fn_x4
ALU = mybir.AluOpType
ACT = mybir.ActivationFunctionType

P = 128
PACK = 4
BLOCKS = D // P
VALS_PLANE = 4
VECTOR_SLOTS = 288


def tile_attend_gbothquestions_kernel(
    tc, query, query2, keys_words, keys_scales, ba, bb, gout, vals_words, vals_scales, fs, keyrows, res, offs, out
):
    nc = tc.nc
    with ExitStack() as ctx:
        sb = ctx.enter_context(tc.tile_pool(name="sb", bufs=1))
        ps = ctx.enter_context(tc.psum_pool(name="ps", bufs=1))

        def tile(name, shape, dtype, slot=None):
            return sb.tile(shape, dtype, name=name, tag=slot or name, align_bytes=64)

        def load_words(name, words, slot):
            pool = tile(name, [P, T], I32, slot)
            nc.sync.dma_start(out=pool[:], in_=words[0].rearrange("p n t -> p (n t)").bitcast(I32))
            return pool

        def load_scales(name, scales, first, slot, clear):
            pool = tile(name, [P, T], U8, slot)
            clear(pool[:].bitcast(I32), 0)
            for r in range(4):
                nc.sync.dma_start(
                    out=pool[first + r : P : 32, :].bitcast(I32),
                    in_=scales[0, r:16:4, :].bitcast(I32),
                )
            return pool

        def load_columns(name, src, slot):
            raw = tile(name, [P, PACK, Q], F32, slot)
            nc.sync.dma_start(out=raw[:], in_=src.rearrange("(p t) q -> p t q", t=PACK))
            return raw

        def load_rows(j, slot):
            rows = tile("row_pool%d" % j, [P, T], F32, slot)
            nc.sync.dma_start(out=rows[:], in_=keyrows[P * j : P * (j + 1), :])
            return rows

        def quantize(name, grouped, slot=None):
            words = grouped.shape[1] // PACK
            codes = tile(name + "_codes", [P, words], U32, slot)
            scales = tile(name + "_scales", [P, words], U8)
            nc.vector.quantize_mx(out=codes[:].bitcast(FP8X4), scales=scales[:], in_=grouped)
            return codes, scales

        def product(dst, lhs_codes, lhs_scales, rhs_codes, rhs_scales):
            nc.tensor.matmul_mx(
                out=dst,
                lhsT=lhs_codes.bitcast(FP8X4),
                lhsT_scale=lhs_scales,
                rhs=rhs_codes.bitcast(FP8X4),
                rhs_scale=rhs_scales,
                start=True,
                stop=True,
            )

        def interleave(dst, raw):
            nc.vector.tensor_copy(
                out=dst.rearrange("p (c i t) -> p c t i", i=4, t=PACK),
                in_=raw[:].rearrange("p t (c i) -> p c t i", i=4),
            )

        def turn_pairs(name, rows, bank_tag, copy, slot):
            bank = ps.tile([P, 2, P], F32, name=name + "_bank", tag=bank_tag)
            words = rows[:].bitcast(F32)
            for u in range(2):
                nc.tensor.transpose(bank[:, u, :], words[:, u : I // 2 : 2], ident[:])
            grouped = tile(name + "_grouped", [P, P * PACK], BF16, slot)
            copy(
                out=grouped[:].bitcast(F32).rearrange("p (c u) -> p c u", u=2),
                in_=bank[:].rearrange("p u c -> p c u"),
            )
            return grouped

        q_raw = load_columns("q_raw", query, "slot_a")
        q2_raw = load_columns("q2_raw", query2, "slot_b")
        g_raw = load_columns("g_raw", gout, "slot_c")
        offsets = sb.tile([P, I // 16], U16, name="offsets")
        nc.sync.dma_start(offsets[:], offs)
        ba_sb = tile("ba_sb", [P, 1], F32)
        bb_sb = tile("bb_sb", [P, 1], F32)
        fs_sb = tile("fs_sb", [P, PACK], F32)
        nc.sync.dma_start(out=ba_sb[:], in_=ba)
        nc.sync.dma_start(out=bb_sb[:], in_=bb)
        key_pool = load_words("key_pool", keys_words, "slot_d")
        nc.sync.dma_start(out=fs_sb[:], in_=fs.rearrange("o (p t) -> p (o t)", t=PACK))
        key_scale_pool = load_scales("key_scale_pool", keys_scales, 0, "slot_e", nc.gpsimd.memset)
        ident = tile("ident", [P, P], F32)
        make_identity(nc, ident[:])

        qq_grouped = tile("qq_grouped", [P, 2 * Q * PACK], BF16, "slot_f")
        g_grouped = tile("g_grouped", [P, Q * PACK], BF16, "slot_g")
        interleave(qq_grouped[:, 0 : Q * PACK], q_raw)
        val_pool = load_words("val_pool", vals_words, "slot_a")
        interleave(qq_grouped[:, Q * PACK : 2 * Q * PACK], q2_raw)
        val_scale_pool = load_scales("val_scale_pool", vals_scales, VALS_PLANE, "slot_b", nc.vector.memset)
        interleave(g_grouped[:], g_raw)
        qq_codes, qq_scales = quantize("qq", qq_grouped[:], "slot_h")
        row_pool = [load_rows(0, "slot_f")]
        g_codes, g_scales = quantize("g", g_grouped[:], "slot_i")
        neg_ba = tile("neg_ba", [P, 1], F32, "slot_j")
        nc.vector.tensor_scalar(neg_ba[:], ba_sb[:], -1.0, None, ALU.mult)

        key_codes = tile("key_codes", [P, I], U32, "slot_c")
        key_scales = tile("key_scales", [P, I], U8, "slot_g")
        nc.vector.tensor_copy(key_codes[:], key_pool[:].bitcast(U32).indirect(offsets[:]))
        row_pool.append(load_rows(1, "slot_d"))
        nc.vector.tensor_copy(key_scales[:], key_scale_pool[:].indirect(offsets[:]))
        a_ps = ps.tile([P, I], F32, name="a_ps", tag="bank_a")
        b_ps = ps.tile([P, I], F32, name="b_ps", tag="bank_b")
        product(a_ps[:], qq_codes[:, 0:Q], qq_scales[:, 0:Q], key_codes[:], key_scales[:])
        product(b_ps[:], qq_codes[:, Q : 2 * Q], qq_scales[:, Q : 2 * Q], key_codes[:], key_scales[:])
        row_pool.append(load_rows(2, "slot_h"))

        fs_ps = ps.tile([P, PACK, P], F32, name="fs_ps")
        for t in range(PACK):
            nc.tensor.transpose(fs_ps[:, t, :], fs_sb[:, t : t + 1].to_broadcast([P, P]), ident[:])

        u1 = tile("u1", [P, I], F32)
        u2 = tile("u2", [P, I], F32)
        rest1 = tile("rest1", [P, I], F32)
        nc.scalar.activation(u1[:], a_ps[:], ACT.Sigmoid, bias=ba_sb[:])
        nc.scalar.activation(u2[:], b_ps[:], ACT.Sigmoid, bias=bb_sb[:])
        nc.scalar.activation(rest1[:], a_ps[:], ACT.Sigmoid, bias=neg_ba[:], scale=-1.0)

        val_codes = tile("val_codes", [P, I], U32)
        val_scales = tile("val_scales", [P, I], U8, "slot_e")
        nc.vector.tensor_copy(val_codes[:], val_pool[:].bitcast(U32).indirect(offsets[:]))
        row_pool.append(load_rows(3, "slot_a"))
        nc.vector.tensor_copy(val_scales[:], val_scale_pool[:].indirect(offsets[:]))
        dp_ps = ps.tile([P, I], F32, name="dp_ps")
        product(dp_ps[:], g_codes[:], g_scales[:], val_codes[:], val_scales[VALS_PLANE:P, :])
        res_sb = tile("res_sb", [P, D], F32, "slot_i")
        nc.sync.dma_start(out=res_sb[:], in_=res)

        pw = tile("pw", [P, I], F32, "slot_b")
        p_sum = tile("p_sum", [P, 1], F32)
        inv_sum = tile("inv_sum", [P, 1], F32)
        p_rest = tile("p_rest", [P, I], F32)
        factor = tile("factor", [P, I], F32, "slot_k")
        w_dp = tile("w_dp", [P, I], F32)
        mean_dp = tile("mean_dp", [P, 1], F32)
        ds = tile("ds", [P, I], BF16, "slot_l")
        nc.vector.scalar_tensor_tensor(pw[:], u1[:], 1.0, u2[:], ALU.mult, ALU.mult, accum_out=p_sum[:])
        nc.vector.tensor_tensor(p_rest[:], pw[:], rest1[:], ALU.mult)
        nc.vector.reciprocal(inv_sum[:], p_sum[:])
        nc.vector.scalar_tensor_tensor(w_dp[:], dp_ps[:], inv_sum[:], pw[:], ALU.mult, ALU.mult, accum_out=mean_dp[:])
        nc.vector.scalar_tensor_tensor(
            factor[:].rearrange("p (s t) -> p s t", t=PACK),
            p_rest[:].rearrange("p (s t) -> p s t", t=PACK),
            inv_sum[:],
            fs_ps[:].rearrange("p t s -> p s t"),
            ALU.mult,
            ALU.mult,
        )
        nc.vector.scalar_tensor_tensor(ds[:], dp_ps[:], mean_dp[:], factor[:], ALU.subtract, ALU.mult)

        def pick_rows(j, slot):
            picked = tile("picked%d" % j, [P, I], BF16, slot)
            if j < BLOCKS - 1:
                nc.scalar.activation(picked[:], row_pool[j][:].indirect(offsets[:]), ACT.Copy)
            else:
                cut = VECTOR_SLOTS // 16
                nc.vector.tensor_copy(picked[:, 0:VECTOR_SLOTS], row_pool[j][:].indirect(offsets[:, 0:cut]))
                nc.scalar.activation(
                    picked[:, VECTOR_SLOTS:I], row_pool[j][:].indirect(offsets[:, cut : I // 16]), ACT.Copy
                )
            return picked

        picked0 = pick_rows(0, "slot_j")
        picked1 = pick_rows(1, "slot_m")
        kt = [quantize("kt0", turn_pairs("kt0", picked0, "bank_x", nc.scalar.copy, "slot_d")[:], "slot_k")]
        kt1_grouped = turn_pairs("kt1", picked1, "bank_y", nc.scalar.copy, "slot_n")
        picked2 = pick_rows(2, "slot_m")
        dt_codes, dt_scales = quantize("dt", turn_pairs("dt", ds, "bank_z", nc.vector.tensor_copy, "slot_l")[:])
        kt.append(quantize("kt1", kt1_grouped[:], "slot_l"))
        picked3 = pick_rows(3, "slot_n")
        kt.append(quantize("kt2", turn_pairs("kt2", picked2, "bank_z", nc.scalar.copy, "slot_a")[:]))
        kt.append(quantize("kt3", turn_pairs("kt3", picked3, "bank_x", nc.scalar.copy, None)[:]))
        y_early = tile("y_early", [P, (BLOCKS - 1) * P], F32)
        y_last = tile("y_last", [P, P], F32)
        groups = [
            (0, 2, "bank_c", y_early[:, 0 : 2 * P]),
            (2, 3, "bank_b", y_early[:, 2 * P : 3 * P]),
            (3, 4, "bank_a", y_last[:]),
        ]
        for first, end, bank_tag, y in groups:
            gq = ps.tile([P, (end - first) * P], F32, name="gq%d" % first, tag=bank_tag)
            for j in range(first, end):
                cols = slice((j - first) * P, (j - first + 1) * P)
                product(gq[:, cols], dt_codes[:], dt_scales[:], kt[j][0][:], kt[j][1][:])
            nc.vector.tensor_tensor(y, gq[:], res_sb[:, first * P : end * P], ALU.add)
        nc.sync.dma_start(out=out[:, 0 : (BLOCKS - 1) * P], in_=y_early[:])
        nc.sync.dma_start(out=out[:, (BLOCKS - 1) * P : D], in_=y_last[:])
